import numpy as np
import ml_dtypes


def mxq(x, axis, fmt="e4m3"):
    dtype, down = {"e4m3": (ml_dtypes.float8_e4m3fn, 7), "e5m2": (ml_dtypes.float8_e5m2, 14)}[fmt]
    v = np.moveaxis(np.asarray(x, np.float32).astype(ml_dtypes.bfloat16).astype(np.float64), axis, -1)
    blocks = v.reshape(v.shape[:-1] + (-1, 32))
    amax = np.abs(blocks).max(-1, keepdims=True)
    byte = np.maximum(np.where(amax > 0, np.frexp(amax)[1] - 1 + 127, 0) - down, 1)
    scale = np.exp2(byte - 127.0)
    codes = (blocks / scale).astype(np.float32).astype(dtype).astype(np.float64)
    return np.moveaxis((codes * scale).reshape(v.shape), -1, axis)


WIDE = False


def mx_kscale(k):
    if not WIDE:
        return np.ones(k)
    levels = np.array([10, -10, 5, -5, 0])
    if k % 512:
        return np.exp2(np.random.permutation(np.resize(levels, k // 32))).repeat(32)
    a = np.empty((k // 512, 16))
    for p in range(k // 512):
        a[p, :8] = np.random.permutation(np.resize(levels, 8))
        for g in range(8):
            far = levels[np.abs(levels - a[p, g]) >= 10]
            a[p, g + 8] = far[np.random.randint(len(far))]
    return np.exp2(a.ravel()).repeat(32)


BF16 = ml_dtypes.bfloat16


def bf(x):
    return np.asarray(x, np.float32).astype(BF16)


def f64(x):
    return np.asarray(x).astype(np.float64)


E2M1 = np.array([0.0, 0.5, 1.0, 1.5, 2.0, 3.0, 4.0, 6.0, -0.0, -0.5, -1.0, -1.5, -2.0, -3.0, -4.0, -6.0])


def pack_weight(w, fmt):
    k, n = w.shape
    w = f64(bf(w)).reshape(k // 32, 32, n)
    amax = np.abs(w).max(1)
    if fmt == "e4m3":
        byte = np.frexp(amax)[1] - 1 + 127 - 7
    else:
        mant, ex = np.frexp(amax / 6.0)
        byte = np.where(mant > 0.5, ex, ex - 1) + 127
    byte = np.clip(np.where(amax > 0, byte, 1), 1, 254)
    scaled = (w * np.exp2(127.0 - byte)[:, None, :]).reshape(k, n).astype(np.float32)
    by_word = np.ascontiguousarray(scaled.reshape(k // 512, 128, 4, n).transpose(0, 1, 3, 2))
    if fmt == "e4m3":
        words = by_word.astype(ml_dtypes.float8_e4m3fn).view(np.uint8)
    else:
        c = by_word.astype(ml_dtypes.float4_e2m1fn).view(np.uint8) & 0xF
        words = c[..., 0::2] | (c[..., 1::2] << 4)
    return np.ascontiguousarray(words), np.ascontiguousarray(byte.astype(np.uint8).reshape(k // 512, 16, n))


def unpack_weight(words, scales, fmt):
    g, p, n, _ = words.shape
    if fmt == "e4m3":
        vals = np.ascontiguousarray(words).view(ml_dtypes.float8_e4m3fn).astype(np.float64)
    else:
        nib = np.empty((g, p, n, 4), np.uint8)
        nib[..., 0::2] = words & 0xF
        nib[..., 1::2] = words >> 4
        vals = E2M1[nib]
    vals = vals * np.repeat(np.exp2(scales.astype(np.float64) - 127.0), 8, axis=1)[..., None]
    return vals.transpose(0, 1, 3, 2).reshape(g * 512, n)
def pack4(w):
    words, scales = pack_weight(w, "e2m1")
    return words.reshape(words.shape[0], 128, -1), scales


def unpack4(words, scales):
    return unpack_weight(words.reshape(words.shape[0], 128, -1, 2), scales, "e2m1")


def planes(Y):
    n, m = Y.shape
    b = f64(bf(Y)).reshape(n // 32, 32, m)
    amax = np.abs(b).max(1)
    byte = np.clip(np.where(amax > 0, np.frexp(amax)[1] - 1 + 127 - 7, 1), 1, 254)
    codes = (b * np.exp2(127.0 - byte)[:, None, :]).reshape(n, m).astype(np.float32).astype(ml_dtypes.float8_e4m3fn).view(np.uint8)
    words = codes.reshape(n // 512, 128, 4, m).transpose(0, 1, 3, 2)
    return np.ascontiguousarray(words), np.ascontiguousarray(byte.astype(np.uint8).reshape(n // 512, 16, m))


B, S, T, D, V = 2, 256, 512, 512, 1024


def setup_inputs():
    a, t = mx_kscale(D), mx_kscale(D)
    h = bf(np.random.standard_normal((B, T, D)) * a)
    wc_words, wc_scales = pack4(np.random.standard_normal((D, D)) / np.sqrt(D) / a[:, None])
    g = bf((1.0 + 0.25 * np.random.standard_normal(D)) * t)
    s = bf(np.random.standard_normal((B, S, D)) / t)
    wo_words, wo_scales = pack4(np.random.standard_normal((D, V)) / np.sqrt(D) * t[:, None])
    bo = bf(0.5 * np.random.standard_normal(V))
    return {"h": h, "wc_words": wc_words, "wc_scales": wc_scales, "g": g, "s": s, "wo_words": wo_words, "wo_scales": wo_scales, "bo": bo}


def copy_keys(h, wc_words, wc_scales, g):
    p = mxq(f64(h), 2, "e4m3") @ unpack4(wc_words, wc_scales)
    return np.tanh(p) * f64(g)


def log_lift(z):
    n = z.shape[-1]
    m = z.max(-1, keepdims=True)
    lse = m + np.log(np.sum(np.exp(z - m), axis=-1, keepdims=True))
    return z - lse + np.log(n)


def core(h, wc_words, wc_scales, g, s, wo_words, wo_scales, bo):
    k = copy_keys(h, wc_words, wc_scales, g)
    sq = mxq(f64(s), 2, "e4m3")
    cp = (sq @ mxq(k, 2, "e4m3").transpose(0, 2, 1)) / np.sqrt(D)
    gen = (sq @ unpack4(wo_words, wo_scales)) + f64(bo)
    z = np.concatenate([gen, cp], axis=-1)
    return log_lift(z)


def reference(h, wc_words, wc_scales, g, s, wo_words, wo_scales, bo):
    R_out = core(h, wc_words, wc_scales, g, s, wo_words, wo_scales, bo)
    words, scales = planes(np.moveaxis(R_out, 2, 0).reshape(1536, -1))
    return R_out, words, scales

@@ -1,0 +1,557 @@
+import math
+from contextlib import ExitStack
+
+import concourse.mybir as mybir
+from concourse.masks import make_identity
+
+B, S, T, D, V = 2, 256, 512, 512, 1024
+NZ = V + T
+FLOPS = 2 * B * (T * D * D + S * D * T + S * D * V)
+
+F32 = mybir.dt.float32
+BF16 = mybir.dt.bfloat16
+I32 = mybir.dt.int32
+U32 = mybir.dt.uint32
+U8 = mybir.dt.uint8
+FP8X4 = mybir.dt.float8_e4m3fn_x4
+FP4X4 = mybir.dt.float4_e2m1fn_x4
+ACT = mybir.ActivationFunctionType
+ALU = mybir.AluOpType
+
+P = 128
+BANK = 512
+GROUPS = NZ // 512
+TILES = B * S // P
+LN2 = math.log(2.0)
+TERMS = 20
+
+
+def tile_copynetjointgeneratecopyloglift_x2_kernel(
+    tc, h, wc_words, wc_scales, g, s, wo_words, wo_scales, bo, out_0, out_1, out_2
+):
+    nc = tc.nc
+    with ExitStack() as ctx:
+        sb = ctx.enter_context(tc.tile_pool(name="sb", bufs=1))
+        psum = ctx.enter_context(tc.psum_pool(name="psum", bufs=8))
+        ctx.enter_context(tc.manual_schedule())
+
+        def keep(name, shape, dtype):
+            return sb.tile(shape, dtype, name=name, align_bytes=64)
+
+        def bank():
+            return psum.tile([P, BANK], F32, name="bank")
+
+        def copy_on(engine, out, in_):
+            if engine == "scalar":
+                nc.scalar.copy(out=out, in_=in_)
+            else:
+                nc.vector.tensor_copy(out=out, in_=in_)
+
+        ident = keep("ident", [P, P], F32)
+        wc_raw = keep("wc_raw", [P, 2 * D], U8)
+        wc_sraw = keep("wc_sraw", [P, D], U8)
+        wc_codes = keep("wc_codes", [P, 2 * D], U8)
+        wc_plane = keep("wc_plane", [P, D], U8)
+        wo_codes = keep("wo_codes", [P, 2 * V], U8)
+        wo_plane = keep("wo_plane", [P, V], U8)
+        g_raw = keep("g_raw", [P, 4], BF16)
+        g4 = keep("g4", [P, 4], F32)
+        bo_raw = keep("bo_raw", [8, P], BF16)
+        bo_rows = keep("bo_rows", [P, P], F32)
+        bo_cols = keep("bo_cols", [P, 8], F32)
+        series = keep("series", [P, TILES, TERMS + 4], F32)
+        count = keep("count", [P, TERMS], F32)
+        inverse = keep("inverse", [P, TERMS], F32)
+        warm = keep("warm", [P, 8], F32)
+        rows = {}
+        for key in [("h", 0, 0), ("h", 0, 1), ("s", 0, 0), ("h", 1, 0), ("h", 1, 1), ("s", 1, 0)]:
+            rows[key] = keep("rows_%s%d%d" % key, [P, 2, D], BF16)
+        grouped = {key: keep("grp_%s%d%d" % key, [P, 1024], BF16) for key in rows}
+        codes = {key: keep("cod_%s%d%d" % key, [P, 256], U32) for key in rows}
+        plane = {key: keep("pln_%s%d%d" % key, [P, 256], U8) for key in rows}
+        th = [keep("th%d" % i, [P, BANK], F32) for i in range(8)]
+        kb = [keep("kb%d" % i, [P, 1024], BF16) for i in range(4)]
+        k_codes = [keep("kc%d" % b, [P, T], U32) for b in range(B)]
+        k_plane = [keep("kp%d" % b, [P, T], U8) for b in range(B)]
+        gen_t = [keep("gent%d" % b, [P, 8, S], F32) for b in range(B)]
+        nz = [keep("nz%d" % i, [P, NZ], F32) for i in range(TILES)]
+        stats = [keep("st%d" % i, [P, 16], F32) for i in range(TILES)]
+        horner = [keep("hn%d" % i, [P, TERMS + 4], F32) for i in range(TILES)]
+        junk = [keep("junk%d" % i, [P, NZ], BF16) for i in range(2)]
+        res = [keep("res%d" % i, [P, NZ], F32) for i in range(TILES)]
+        res_b = [keep("resb%d" % i, [P, NZ], BF16) for i in range(TILES)]
+        res_g = [keep("resg%d" % i, [P, NZ], BF16) for i in range(TILES)]
+        o_codes = keep("o_codes", [P, GROUPS, B * S], U32)
+        o_plane = keep("o_plane", [P, GROUPS, B * S], U8)
+        banks = {}
+
+        def load_rows(key):
+            name, b, half = key
+            src = h[b, 256 * half : 256 * half + 256, :] if name == "h" else s[b]
+            nc.sync.dma_start(out=rows[key][:], in_=src.rearrange("(j p) d -> p j d", p=P))
+
+        def load_scale_rows(engine, dst, src):
+            for q in range(4):
+                engine.dma_start(
+                    out=dst[32 * q : 32 * q + 4, :].bitcast(I32),
+                    in_=src[0, 4 * q : 4 * q + 4, :].bitcast(I32),
+                )
+
+        def turn_rows(key):
+            banks[key] = bank()
+            for j in range(2):
+                words = rows[key][:, j, :].bitcast(F32)
+                for u in range(2):
+                    c0 = (2 * j + u) * P
+                    nc.tensor.transpose(banks[key][:, c0 : c0 + P], words[:, u::2], ident[:])
+
+        def copy_rows(key, engine):
+            copy_on(
+                engine,
+                grouped[key][:].bitcast(F32).rearrange("p (j r u) -> p j r u", j=2, u=2),
+                banks[key][:].rearrange("p (j u r) -> p j r u", j=2, u=2),
+            )
+
+        def quant_rows(key):
+            nc.vector.quantize_mx(out=codes[key][:].bitcast(FP8X4), scales=plane[key][:], in_=grouped[key][:])
+
+        def project(b, j):
+            key = ("h", b, j // 2)
+            cols = slice((j % 2) * P, (j % 2) * P + P)
+            banks["p", b, j] = bank()
+            for t in range(4):
+                nc.tensor.matmul_mx(
+                    out=banks["p", b, j][:, t * P : (t + 1) * P],
+                    lhsT=wc_codes[:, 2 * P * t : 2 * P * (t + 1)].bitcast(FP4X4),
+                    lhsT_scale=wc_plane[:, P * t : P * (t + 1)],
+                    rhs=codes[key][:, cols].bitcast(FP8X4),
+                    rhs_scale=plane[key][:, cols],
+                    start=True,
+                    stop=True,
+                )
+
+        def squash(b, j):
+            nc.scalar.activation(
+                out=th[4 * b + j][:].rearrange("p (n t) -> p n t", t=4),
+                in_=banks["p", b, j][:].rearrange("p (t n) -> p n t", t=4),
+                func=ACT.Tanh,
+            )
+
+        def gain(b, j, engine="vector"):
+            c0 = (j % 2) * BANK
+            (nc.vector if engine == "vector" else nc.gpsimd).tensor_tensor(
+                out=kb[2 * b + j // 2][:, c0 : c0 + BANK].rearrange("p (n t) -> p n t", t=4),
+                in0=th[4 * b + j][:].rearrange("p (n t) -> p n t", t=4),
+                in1=g4[:].unsqueeze(1).to_broadcast([P, P, 4]),
+                op=ALU.mult,
+            )
+
+        def quant_keys(b, half):
+            cols = slice(256 * half, 256 * half + 256)
+            nc.vector.quantize_mx(
+                out=k_codes[b][:, cols].bitcast(FP8X4), scales=k_plane[b][:, cols], in_=kb[2 * b + half][:]
+            )
+
+        def generate(b, pair):
+            key = ("s", b, 0)
+            banks["g", b, pair] = bank()
+            for e in range(2):
+                c = 2 * pair + e
+                nc.tensor.matmul_mx(
+                    out=banks["g", b, pair][:, e * S : (e + 1) * S],
+                    lhsT=wo_codes[:, 2 * P * c : 2 * P * (c + 1)].bitcast(FP4X4),
+                    lhsT_scale=wo_plane[:, P * c : P * (c + 1)],
+                    rhs=codes[key][:].bitcast(FP8X4),
+                    rhs_scale=plane[key][:],
+                    start=True,
+                    stop=True,
+                )
+
+        def add_bias(b, c, engine="scalar"):
+            src = banks["g", b, c // 2][:, (c % 2) * S : (c % 2 + 1) * S]
+            if engine == "scalar":
+                nc.scalar.activation(out=gen_t[b][:, c, :], in_=src, func=ACT.Identity, bias=bo_cols[:, c : c + 1])
+            else:
+                nc.vector.tensor_scalar(
+                    out=gen_t[b][:, c, :], in0=src, scalar1=bo_cols[:, c : c + 1], scalar2=None, op0=ALU.add
+                )
+
+        def turn_scores(i, half):
+            b, r0 = i // 2, (i % 2) * P
+            banks["z", i, half] = bank()
+            for e in range(4):
+                nc.tensor.transpose(
+                    banks["z", i, half][:, e * P : (e + 1) * P], gen_t[b][:, 4 * half + e, r0 : r0 + P], ident[:]
+                )
+
+        def copy_scores(i):
+            b = i // 2
+            cols = slice((i % 2) * P, (i % 2) * P + P)
+            banks["z", i, 2] = bank()
+            nc.tensor.matmul_mx(
+                out=banks["z", i, 2][:],
+                lhsT=codes["s", b, 0][:, cols].bitcast(FP8X4),
+                lhsT_scale=plane["s", b, 0][:, cols],
+                rhs=k_codes[b][:].bitcast(FP8X4),
+                rhs_scale=k_plane[b][:],
+                start=True,
+                stop=True,
+            )
+
+        def negate_min(i, part, col):
+            factor = -1.0 / math.sqrt(D) if part == 2 else -1.0
+            nc.vector.tensor_scalar(
+                out=nz[i][:, part * BANK : (part + 1) * BANK],
+                in0=banks["z", i, part][:],
+                scalar1=factor,
+                scalar2=None if col == 0 else stats[i][:, col - 1 : col],
+                op0=ALU.mult,
+                op1=ALU.min,
+                accum_out=stats[i][:, col : col + 1],
+            )
+
+        def exp_sum(i):
+            nc.scalar.activation(
+                out=junk[i % 2][:],
+                in_=nz[i][:],
+                func=ACT.Exp,
+                scale=-1.0,
+                bias=stats[i][:, 2:3],
+                accum_out=stats[i][:, 3:4],
+            )
+
+        def log_guess(i):
+            nc.scalar.activation(
+                out=stats[i][:, 4:5],
+                in_=stats[i][:, 3:4].bitcast(U32),
+                func=ACT.Copy,
+                scale=-LN2 / 2.0**23,
+                bias=(127.0 - 0.043) * LN2,
+            )
+
+        def log_ratio(i):
+            nc.scalar.activation(out=stats[i][:, 5:6], in_=stats[i][:, 4:5], func=ACT.Exp)
+
+        def log_base(i):
+            nc.vector.tensor_scalar(
+                out=series[:, i, TERMS : TERMS + 1],
+                in0=stats[i][:, 4:5],
+                scalar1=stats[i][:, 2:3],
+                scalar2=math.log(NZ),
+                op0=ALU.add,
+                op1=ALU.add,
+            )
+
+        def log_eps(i):
+            nc.vector.tensor_scalar(
+                out=stats[i][:, 6:7],
+                in0=stats[i][:, 3:4],
+                scalar1=stats[i][:, 5:6],
+                scalar2=-1.0,
+                op0=ALU.mult,
+                op1=ALU.add,
+            )
+
+        def log_series(i):
+            nc.vector.tensor_tensor_scan(
+                out=horner[i][:, 0 : TERMS + 1],
+                data0=stats[i][:, 6:7].to_broadcast([P, TERMS + 1]),
+                data1=series[:, i, 0 : TERMS + 1],
+                initial=0.0,
+                op0=ALU.mult,
+                op1=ALU.add,
+            )
+
+        def lift(engine, dst, i, cols):
+            if engine == "scalar":
+                nc.scalar.activation(
+                    out=dst[i][:, cols], in_=nz[i][:, cols], func=ACT.Identity, scale=-1.0, bias=horner[i][:, TERMS : TERMS + 1]
+                )
+            else:
+                (nc.vector if engine == "vector" else nc.gpsimd).tensor_scalar(
+                    out=dst[i][:, cols],
+                    in0=nz[i][:, cols],
+                    scalar1=-1.0,
+                    scalar2=horner[i][:, TERMS : TERMS + 1],
+                    op0=ALU.mult,
+                    op1=ALU.add,
+                )
+
+        def store_result(i, cols):
+            nc.sync.dma_start(out=out_0[i // 2, (i % 2) * P : (i % 2) * P + P, cols], in_=res[i][:, cols])
+
+        def turn_result(i, first, count):
+            banks["o", i, first] = bank()
+            words = res_b[i][:].bitcast(F32)
+            for gg in range(count):
+                for u in range(2):
+                    c0 = (2 * gg + u) * P
+                    w0 = 256 * (first + gg)
+                    nc.tensor.transpose(
+                        banks["o", i, first][:, c0 : c0 + P], words[:, w0 + u : w0 + 256 : 2], ident[:]
+                    )
+
+        def copy_result(i, first, count, engine):
+            copy_on(
+                engine,
+                res_g[i][:, 512 * first : 512 * (first + count)]
+                .bitcast(F32)
+                .rearrange("p (j r u) -> p j r u", j=count, u=2),
+                banks["o", i, first][:, 0 : 256 * count].rearrange("p (j u r) -> p j r u", j=count, u=2),
+            )
+
+        def quant_result(i, gg):
+            cols = slice(i * P, i * P + P)
+            nc.vector.quantize_mx(
+                out=o_codes[:, gg, cols].bitcast(FP8X4),
+                scales=o_plane[:, gg, cols],
+                in_=res_g[i][:, 512 * gg : 512 * (gg + 1)],
+            )
+
+        def store_codes(first, count):
+            cols = slice(first * P, (first + count) * P)
+            dst = out_1.rearrange("g p m t -> p g (m t)").bitcast(I32)
+            nc.sync.dma_start(out=dst[:, :, cols], in_=o_codes[:, :, cols].bitcast(I32))
+
+        def store_scales(q, engine):
+            engine.dma_start(
+                out=out_2[:, 4 * q : 4 * q + 4, :].rearrange("g r m -> r g m").bitcast(I32),
+                in_=o_plane[32 * q : 32 * q + 4, :, :].bitcast(I32),
+            )
+
+        ALL = slice(0, NZ)
+        H0A, H0B, S0, H1A, H1B, S1 = list(rows)
+
+        nc.vector.memset(warm[:], 0.0)
+        nc.scalar.activation(out=warm[:, 4:5], in_=warm[:, 0:1], func=ACT.Tanh)
+        nc.vector.memset(wc_sraw[:].bitcast(I32), 0)
+        nc.vector.memset(wo_plane[:].bitcast(I32), 0)
+        nc.vector.memset(bo_rows[:], 0.0)
+        load_rows(H0A)
+        nc.sync.dma_start(out=wc_raw[:].bitcast(I32), in_=wc_words[0].bitcast(I32))
+        load_scale_rows(nc.sync, wc_sraw, wc_scales)
+        load_rows(H0B)
+        load_rows(S0)
+        nc.sync.dma_start(out=wo_codes[:].bitcast(I32), in_=wo_words[0].bitcast(I32))
+        load_scale_rows(nc.sync, wo_plane, wo_scales)
+        load_rows(H1A)
+        load_rows(H1B)
+        load_rows(S1)
+        nc.gpsimd.dma_start(out=bo_raw[:], in_=bo.rearrange("(c p) -> c p", p=P))
+        make_identity(nc, ident[:])
+        nc.gpsimd.iota(
+            count[:], pattern=[[-1, TERMS]], base=TERMS, channel_multiplier=0, allow_small_or_imprecise_dtypes=True
+        )
+        nc.gpsimd.dma_start(out=g_raw[:], in_=g.rearrange("(p t) -> p t", t=4))
+
+        nc.vector.tensor_copy(
+            out=wc_codes[:].rearrange("p (t m e) -> p t m e", t=4, e=2),
+            in_=wc_raw[:].rearrange("p (m t e) -> p t m e", t=4, e=2),
+        )
+        nc.vector.tensor_copy(
+            out=wc_plane[:].rearrange("p (t m) -> p t m", t=4),
+            in_=wc_sraw[:].rearrange("p (m t) -> p t m", t=4),
+        )
+
+        def fill_series():
+            nc.vector.reciprocal(out=inverse[:], in_=count[:])
+
+        def sign_series():
+            for first, factor in [(0, 1.0), (1, -1.0)]:
+                nc.vector.tensor_scalar(
+                    out=series[:, :, first:TERMS:2],
+                    in0=inverse[:, first:TERMS:2].unsqueeze(1).to_broadcast([P, TILES, TERMS // 2]),
+                    scalar1=factor,
+                    scalar2=None,
+                    op0=ALU.mult,
+                )
+
+        def cast_bias():
+            nc.vector.tensor_copy(out=bo_rows[0:8, :], in_=bo_raw[:])
+
+        def turn_bias():
+            banks["bo"] = bank()
+            nc.tensor.transpose(banks["bo"][:, 0:P], bo_rows[:], ident[:])
+
+        def copy_bias():
+            nc.vector.tensor_copy(out=bo_cols[:], in_=banks["bo"][:, 0:8])
+
+        def copy_gain():
+            nc.vector.tensor_copy(out=g4[:], in_=g_raw[:])
+
+        turn_rows(H0A)
+        copy_rows(H0A, "scalar")
+        cast_bias()
+        fill_series()
+        turn_rows(H0B)
+        turn_bias()
+        quant_rows(H0A)
+        copy_rows(H0B, "vector")
+        turn_rows(S0)
+        project(0, 0)
+        project(0, 1)
+        copy_rows(S0, "scalar")
+        copy_bias()
+        sign_series()
+        quant_rows(H0B)
+        project(0, 2)
+        project(0, 3)
+        copy_gain()
+        quant_rows(S0)
+        squash(0, 0)
+        generate(0, 0)
+        generate(0, 1)
+        squash(0, 1)
+        gain(0, 0)
+        generate(0, 2)
+        generate(0, 3)
+        squash(0, 2)
+        gain(0, 1)
+        turn_rows(H1A)
+        squash(0, 3)
+        turn_rows(H1B)
+        gain(0, 2)
+        quant_keys(0, 0)
+        gain(0, 3)
+        turn_rows(S1)
+        add_bias(0, 0)
+        add_bias(0, 1)
+        add_bias(0, 2)
+        add_bias(0, 3)
+        copy_rows(H1A, "vector")
+        quant_keys(0, 1)
+        turn_scores(0, 0)
+        turn_scores(1, 0)
+        quant_rows(H1A)
+        copy_scores(0)
+        add_bias(0, 4)
+        add_bias(0, 5)
+        add_bias(0, 6)
+        add_bias(0, 7)
+        project(1, 0)
+        negate_min(0, 0, 0)
+        project(1, 1)
+        copy_rows(H1B, "scalar")
+        turn_scores(0, 1)
+        negate_min(1, 0, 0)
+        copy_rows(S1, "scalar")
+        turn_scores(1, 1)
+        negate_min(0, 2, 1)
+        quant_rows(H1B)
+        copy_scores(1)
+        squash(1, 0)
+        project(1, 2)
+        project(1, 3)
+        negate_min(0, 1, 2)
+        quant_rows(S1)
+        squash(1, 1)
+        exp_sum(0)
+        negate_min(1, 2, 1)
+        gain(1, 0)
+        negate_min(1, 1, 2)
+        gain(1, 1)
+        generate(1, 0)
+        generate(1, 1)
+        generate(1, 2)
+        generate(1, 3)
+        squash(1, 2)
+        log_guess(0)
+        squash(1, 3)
+        log_ratio(0)
+        add_bias(1, 0)
+        add_bias(1, 1)
+        add_bias(1, 2)
+        add_bias(1, 3)
+        turn_scores(2, 0)
+        turn_scores(3, 0)
+        exp_sum(1)
+        gain(1, 2)
+        quant_keys(1, 0)
+        gain(1, 3)
+        log_base(0)
+        log_eps(0)
+        quant_keys(1, 1)
+        log_series(0)
+        copy_scores(2)
+        copy_scores(3)
+        negate_min(2, 0, 0)
+        lift("vector", res_b, 0, ALL)
+        turn_result(0, 0, 2)
+        turn_result(0, 2, 1)
+        add_bias(1, 4)
+        log_guess(1)
+        add_bias(1, 5)
+        log_ratio(1)
+        add_bias(1, 6)
+        add_bias(1, 7)
+        turn_scores(2, 1)
+        turn_scores(3, 1)
+        negate_min(2, 2, 1)
+        lift("vector", res, 0, ALL)
+        store_result(0, ALL)
+        log_base(1)
+        log_eps(1)
+        negate_min(2, 1, 2)
+        log_series(1)
+        negate_min(3, 0, 0)
+        copy_result(0, 0, 2, "scalar")
+        copy_result(0, 2, 1, "scalar")
+        exp_sum(2)
+        lift("vector", res, 1, slice(0, 768))
+        negate_min(3, 2, 1)
+        lift("vector", res, 1, slice(768, NZ))
+        store_result(1, ALL)
+        negate_min(3, 1, 2)
+        log_guess(2)
+        log_ratio(2)
+        exp_sum(3)
+        lift("vector", res_b, 1, ALL)
+        turn_result(1, 0, 2)
+        turn_result(1, 2, 1)
+        log_base(2)
+        log_eps(2)
+        quant_result(0, 0)
+        log_series(2)
+        quant_result(0, 1)
+        lift("vector", res, 2, ALL)
+        store_result(2, ALL)
+        quant_result(0, 2)
+        store_codes(0, 1)
+        log_guess(3)
+        copy_result(1, 2, 1, "scalar")
+        log_ratio(3)
+        copy_result(1, 0, 2, "scalar")
+        lift("vector", res_b, 2, slice(0, 1024))
+        log_base(3)
+        log_eps(3)
+        lift("vector", res_b, 2, slice(1024, NZ))
+        log_series(3)
+        turn_result(2, 0, 2)
+        turn_result(2, 2, 1)
+        quant_result(1, 2)
+        lift("scalar", res, 3, slice(0, 768))
+        store_result(3, slice(0, 768))
+        lift("vector", res_b, 3, slice(0, 1024))
+        turn_result(3, 0, 2)
+        lift("vector", res_b, 3, slice(1024, NZ))
+        turn_result(3, 2, 1)
+        lift("vector", res, 3, slice(768, NZ))
+        store_result(3, slice(768, NZ))
+        copy_result(2, 0, 2, "scalar")
+        copy_result(3, 0, 2, "scalar")
+        quant_result(1, 0)
+        quant_result(1, 1)
+        store_codes(1, 1)
+        copy_result(2, 2, 1, "vector")
+        quant_result(2, 0)
+        copy_result(3, 2, 1, "vector")
+        quant_result(2, 1)
+        quant_result(2, 2)
+        quant_result(3, 2)
+        quant_result(3, 0)
+        quant_result(3, 1)
+        store_codes(2, 2)
+        store_scales(0, nc.scalar)
+        store_scales(1, nc.sync)
+        store_scales(2, nc.scalar)
+        store_scales(3, nc.sync)

@@ -62,7 +62,8 @@ def tile_copynetjointgeneratecopyloglift_x2_kernel(
         series = keep("series", [P, TILES, TERMS + 4], F32)
         count = keep("count", [P, TERMS], F32)
         inverse = keep("inverse", [P, TERMS], F32)
-        warm = keep("warm", [P, 8], F32)
+        warm = keep("warm", [P, P], F32)
+        table = keep("table", [P, 8], F32)
         rows = {}
         for key in [("h", 0, 0), ("h", 0, 1), ("s", 0, 0), ("h", 1, 0), ("h", 1, 1), ("s", 1, 0)]:
             rows[key] = keep("rows_%s%d%d" % key, [P, 2, D], BF16)
@@ -277,6 +278,21 @@ def tile_copynetjointgeneratecopyloglift_x2_kernel(
                     op1=ALU.add,
                 )
 
+        def round_result(i, first, count):
+            for gg in range(first, first + count):
+                cols = slice(512 * gg, 512 * (gg + 1))
+                nc.vector.tensor_scalar(
+                    out=res_b[i][:, cols].rearrange("p (u w e) -> p u w e", u=2, e=2),
+                    in0=nz[i][:, cols].rearrange("p (w u e) -> p u w e", u=2, e=2),
+                    scalar1=-1.0,
+                    scalar2=horner[i][:, TERMS : TERMS + 1],
+                    op0=ALU.mult,
+                    op1=ALU.add,
+                )
+
+        def keep_warm(src):
+            nc.tensor.matmul(out=banks["warm"][:, 0:P], lhsT=warm[:], rhs=src, start=True, stop=True)
+
         def store_result(i, cols):
             nc.sync.dma_start(out=out_0[i // 2, (i % 2) * P : (i % 2) * P + P, cols], in_=res[i][:, cols])
 
@@ -288,7 +304,7 @@ def tile_copynetjointgeneratecopyloglift_x2_kernel(
                     c0 = (2 * gg + u) * P
                     w0 = 256 * (first + gg)
                     nc.tensor.transpose(
-                        banks["o", i, first][:, c0 : c0 + P], words[:, w0 + u : w0 + 256 : 2], ident[:]
+                        banks["o", i, first][:, c0 : c0 + P], words[:, w0 + u * P : w0 + (u + 1) * P], ident[:]
                     )
 
         def copy_result(i, first, count, engine):
@@ -323,7 +339,7 @@ def tile_copynetjointgeneratecopyloglift_x2_kernel(
         H0A, H0B, S0, H1A, H1B, S1 = list(rows)
 
         nc.vector.memset(warm[:], 0.0)
-        nc.scalar.activation(out=warm[:, 4:5], in_=warm[:, 0:1], func=ACT.Tanh)
+        nc.scalar.activation(out=table[:, 0:1], in_=warm[:, 0:1], func=ACT.Tanh)
         nc.vector.memset(wc_sraw[:].bitcast(I32), 0)
         nc.vector.memset(wo_plane[:].bitcast(I32), 0)
         nc.vector.memset(bo_rows[:], 0.0)
@@ -333,16 +349,16 @@ def tile_copynetjointgeneratecopyloglift_x2_kernel(
         load_rows(H0B)
         load_rows(S0)
         nc.sync.dma_start(out=wo_codes[:].bitcast(I32), in_=wo_words[0].bitcast(I32))
+        nc.sync.dma_start(out=g_raw[:], in_=g.rearrange("(p t) -> p t", t=4))
         load_scale_rows(nc.sync, wo_plane, wo_scales)
+        nc.sync.dma_start(out=bo_raw[:], in_=bo.rearrange("(c p) -> c p", p=P))
         load_rows(H1A)
         load_rows(H1B)
         load_rows(S1)
-        nc.gpsimd.dma_start(out=bo_raw[:], in_=bo.rearrange("(c p) -> c p", p=P))
         make_identity(nc, ident[:])
         nc.gpsimd.iota(
             count[:], pattern=[[-1, TERMS]], base=TERMS, channel_multiplier=0, allow_small_or_imprecise_dtypes=True
         )
-        nc.gpsimd.dma_start(out=g_raw[:], in_=g.rearrange("(p t) -> p t", t=4))
 
         nc.vector.tensor_copy(
             out=wc_codes[:].rearrange("p (t m e) -> p t m e", t=4, e=2),
@@ -379,41 +395,47 @@ def tile_copynetjointgeneratecopyloglift_x2_kernel(
         def copy_gain():
             nc.vector.tensor_copy(out=g4[:], in_=g_raw[:])
 
+        banks["warm"] = bank()
+        keep_warm(warm[:])
+        keep_warm(warm[:])
+        keep_warm(warm[:])
+        keep_warm(warm[:])
         turn_rows(H0A)
+        keep_warm(warm[:])
         copy_rows(H0A, "scalar")
-        cast_bias()
         fill_series()
         turn_rows(H0B)
-        turn_bias()
+        keep_warm(warm[:])
         quant_rows(H0A)
         copy_rows(H0B, "vector")
         turn_rows(S0)
         project(0, 0)
         project(0, 1)
         copy_rows(S0, "scalar")
-        copy_bias()
         sign_series()
         quant_rows(H0B)
         project(0, 2)
         project(0, 3)
         copy_gain()
+        cast_bias()
         quant_rows(S0)
+        turn_bias()
         squash(0, 0)
         generate(0, 0)
         generate(0, 1)
         squash(0, 1)
         gain(0, 0)
-        generate(0, 2)
-        generate(0, 3)
-        squash(0, 2)
-        gain(0, 1)
+        copy_bias()
         turn_rows(H1A)
+        squash(0, 2)
+        generate(0, 2)
+        gain(0, 1)
         squash(0, 3)
         turn_rows(H1B)
+        generate(0, 3)
         gain(0, 2)
         quant_keys(0, 0)
         gain(0, 3)
-        turn_rows(S1)
         add_bias(0, 0)
         add_bias(0, 1)
         add_bias(0, 2)
@@ -421,6 +443,7 @@ def tile_copynetjointgeneratecopyloglift_x2_kernel(
         copy_rows(H1A, "vector")
         quant_keys(0, 1)
         turn_scores(0, 0)
+        turn_rows(S1)
         turn_scores(1, 0)
         quant_rows(H1A)
         copy_scores(0)
@@ -454,15 +477,19 @@ def tile_copynetjointgeneratecopyloglift_x2_kernel(
         generate(1, 1)
         generate(1, 2)
         generate(1, 3)
+        banks["warm"] = bank()
+        keep_warm(nz[1][:, 512:640])
         squash(1, 2)
         log_guess(0)
         squash(1, 3)
         log_ratio(0)
         add_bias(1, 0)
+        keep_warm(gen_t[1][:, 0, 0:P])
         add_bias(1, 1)
         add_bias(1, 2)
         add_bias(1, 3)
         turn_scores(2, 0)
+        keep_warm(warm[:])
         turn_scores(3, 0)
         exp_sum(1)
         gain(1, 2)
@@ -475,7 +502,7 @@ def tile_copynetjointgeneratecopyloglift_x2_kernel(
         copy_scores(2)
         copy_scores(3)
         negate_min(2, 0, 0)
-        lift("vector", res_b, 0, ALL)
+        round_result(0, 0, 3)
         turn_result(0, 0, 2)
         turn_result(0, 2, 1)
         add_bias(1, 4)
@@ -485,6 +512,7 @@ def tile_copynetjointgeneratecopyloglift_x2_kernel(
         add_bias(1, 6)
         add_bias(1, 7)
         turn_scores(2, 1)
+        keep_warm(warm[:])
         turn_scores(3, 1)
         negate_min(2, 2, 1)
         lift("vector", res, 0, ALL)
@@ -492,6 +520,7 @@ def tile_copynetjointgeneratecopyloglift_x2_kernel(
         log_base(1)
         log_eps(1)
         negate_min(2, 1, 2)
+        keep_warm(nz[2][:, 512:640])
         log_series(1)
         negate_min(3, 0, 0)
         copy_result(0, 0, 2, "scalar")
@@ -499,15 +528,18 @@ def tile_copynetjointgeneratecopyloglift_x2_kernel(
         exp_sum(2)
         lift("vector", res, 1, slice(0, 768))
         negate_min(3, 2, 1)
+        keep_warm(nz[3][:, 1024:1152])
         lift("vector", res, 1, slice(768, NZ))
         store_result(1, ALL)
         negate_min(3, 1, 2)
+        keep_warm(nz[3][:, 512:640])
         log_guess(2)
         log_ratio(2)
         exp_sum(3)
-        lift("vector", res_b, 1, ALL)
+        round_result(1, 0, 3)
         turn_result(1, 0, 2)
         turn_result(1, 2, 1)
+        keep_warm(warm[:])
         log_base(2)
         log_eps(2)
         quant_result(0, 0)
@@ -515,25 +547,27 @@ def tile_copynetjointgeneratecopyloglift_x2_kernel(
         quant_result(0, 1)
         lift("vector", res, 2, ALL)
         store_result(2, ALL)
+        keep_warm(res[2][:, 0:P])
         quant_result(0, 2)
         store_codes(0, 1)
         log_guess(3)
         copy_result(1, 2, 1, "scalar")
         log_ratio(3)
         copy_result(1, 0, 2, "scalar")
-        lift("vector", res_b, 2, slice(0, 1024))
+        round_result(2, 0, 2)
         log_base(3)
         log_eps(3)
-        lift("vector", res_b, 2, slice(1024, NZ))
+        round_result(2, 2, 1)
         log_series(3)
         turn_result(2, 0, 2)
         turn_result(2, 2, 1)
+        keep_warm(warm[:])
         quant_result(1, 2)
         lift("scalar", res, 3, slice(0, 768))
         store_result(3, slice(0, 768))
-        lift("vector", res_b, 3, slice(0, 1024))
+        round_result(3, 0, 2)
         turn_result(3, 0, 2)
-        lift("vector", res_b, 3, slice(1024, NZ))
+        round_result(3, 2, 1)
         turn_result(3, 2, 1)
         lift("vector", res, 3, slice(768, NZ))
         store_result(3, slice(768, NZ))

@@ -340,8 +340,9 @@ def tile_copynetjointgeneratecopyloglift_x2_kernel(
 
         nc.vector.memset(warm[:], 0.0)
         nc.scalar.activation(out=table[:, 0:1], in_=warm[:, 0:1], func=ACT.Tanh)
-        nc.vector.memset(wc_sraw[:].bitcast(I32), 0)
-        nc.vector.memset(wo_plane[:].bitcast(I32), 0)
+        nc.gpsimd.memset(wc_sraw[:].bitcast(I32), 0)
+        make_identity(nc, ident[:])
+        nc.gpsimd.memset(wo_plane[:].bitcast(I32), 0)
         nc.vector.memset(bo_rows[:], 0.0)
         load_rows(H0A)
         nc.sync.dma_start(out=wc_raw[:].bitcast(I32), in_=wc_words[0].bitcast(I32))
@@ -355,7 +356,6 @@ def tile_copynetjointgeneratecopyloglift_x2_kernel(
         load_rows(H1A)
         load_rows(H1B)
         load_rows(S1)
-        make_identity(nc, ident[:])
         nc.gpsimd.iota(
             count[:], pattern=[[-1, TERMS]], base=TERMS, channel_multiplier=0, allow_small_or_imprecise_dtypes=True
         )
@@ -405,7 +405,6 @@ def tile_copynetjointgeneratecopyloglift_x2_kernel(
         copy_rows(H0A, "scalar")
         fill_series()
         turn_rows(H0B)
-        keep_warm(warm[:])
         quant_rows(H0A)
         copy_rows(H0B, "vector")
         turn_rows(S0)
@@ -442,149 +441,150 @@ def tile_copynetjointgeneratecopyloglift_x2_kernel(
         add_bias(0, 3)
         copy_rows(H1A, "vector")
         quant_keys(0, 1)
-        turn_scores(0, 0)
         turn_rows(S1)
-        turn_scores(1, 0)
+        turn_scores(0, 0)
         quant_rows(H1A)
+        copy_rows(H1B, "vector")
+        project(1, 0)
+        project(1, 1)
         copy_scores(0)
         add_bias(0, 4)
         add_bias(0, 5)
         add_bias(0, 6)
         add_bias(0, 7)
-        project(1, 0)
-        negate_min(0, 0, 0)
-        project(1, 1)
-        copy_rows(H1B, "scalar")
-        turn_scores(0, 1)
-        negate_min(1, 0, 0)
         copy_rows(S1, "scalar")
-        turn_scores(1, 1)
-        negate_min(0, 2, 1)
+        turn_scores(0, 1)
+        negate_min(0, 0, 0)
         quant_rows(H1B)
-        copy_scores(1)
-        squash(1, 0)
         project(1, 2)
         project(1, 3)
-        negate_min(0, 1, 2)
+        negate_min(0, 2, 1)
         quant_rows(S1)
+        squash(1, 0)
         squash(1, 1)
-        exp_sum(0)
-        negate_min(1, 2, 1)
-        gain(1, 0)
-        negate_min(1, 1, 2)
-        gain(1, 1)
+        turn_scores(1, 0)
         generate(1, 0)
         generate(1, 1)
+        squash(1, 2)
+        squash(1, 3)
+        gain(1, 0)
+        negate_min(0, 1, 2)
         generate(1, 2)
         generate(1, 3)
-        banks["warm"] = bank()
-        keep_warm(nz[1][:, 512:640])
-        squash(1, 2)
-        log_guess(0)
-        squash(1, 3)
-        log_ratio(0)
-        add_bias(1, 0)
-        keep_warm(gen_t[1][:, 0, 0:P])
-        add_bias(1, 1)
-        add_bias(1, 2)
-        add_bias(1, 3)
-        turn_scores(2, 0)
-        keep_warm(warm[:])
-        turn_scores(3, 0)
-        exp_sum(1)
+        copy_scores(1)
+        turn_scores(1, 1)
+        exp_sum(0)
+        gain(1, 1)
         gain(1, 2)
         quant_keys(1, 0)
         gain(1, 3)
+        negate_min(1, 0, 0)
+        quant_keys(1, 1)
+        add_bias(1, 0)
+        log_guess(0)
+        add_bias(1, 1)
+        log_ratio(0)
+        add_bias(1, 2)
+        add_bias(1, 3)
+        copy_scores(2)
+        turn_scores(2, 0)
+        turn_scores(3, 0)
         log_base(0)
         log_eps(0)
-        quant_keys(1, 1)
+        negate_min(1, 2, 1)
         log_series(0)
-        copy_scores(2)
         copy_scores(3)
-        negate_min(2, 0, 0)
-        round_result(0, 0, 3)
-        turn_result(0, 0, 2)
-        turn_result(0, 2, 1)
+        lift("gpsimd", res, 0, ALL)
+        store_result(0, ALL)
         add_bias(1, 4)
-        log_guess(1)
         add_bias(1, 5)
-        log_ratio(1)
         add_bias(1, 6)
         add_bias(1, 7)
         turn_scores(2, 1)
-        keep_warm(warm[:])
         turn_scores(3, 1)
+        banks["warm"] = bank()
+        negate_min(1, 1, 2)
+        exp_sum(1)
+        negate_min(2, 0, 0)
+        keep_warm(nz[2][:, 0:P])
+        negate_min(3, 0, 0)
         negate_min(2, 2, 1)
-        lift("vector", res, 0, ALL)
-        store_result(0, ALL)
-        log_base(1)
-        log_eps(1)
+        keep_warm(nz[2][:, 1024:1152])
+        round_result(0, 0, 1)
         negate_min(2, 1, 2)
         keep_warm(nz[2][:, 512:640])
-        log_series(1)
-        negate_min(3, 0, 0)
-        copy_result(0, 0, 2, "scalar")
-        copy_result(0, 2, 1, "scalar")
+        log_guess(1)
+        log_ratio(1)
         exp_sum(2)
-        lift("vector", res, 1, slice(0, 768))
+        round_result(0, 1, 1)
+        log_base(1)
+        log_eps(1)
+        round_result(0, 2, 1)
+        log_series(1)
+        turn_result(0, 0, 2)
+        turn_result(0, 2, 1)
+        lift("gpsimd", res, 1, ALL)
+        store_result(1, ALL)
         negate_min(3, 2, 1)
         keep_warm(nz[3][:, 1024:1152])
-        lift("vector", res, 1, slice(768, NZ))
-        store_result(1, ALL)
+        copy_result(0, 0, 2, "vector")
         negate_min(3, 1, 2)
         keep_warm(nz[3][:, 512:640])
         log_guess(2)
+        copy_result(0, 2, 1, "scalar")
         log_ratio(2)
         exp_sum(3)
-        round_result(1, 0, 3)
+        log_base(2)
+        log_eps(2)
+        round_result(1, 0, 1)
+        log_series(2)
+        round_result(1, 1, 1)
+        lift("vector", res, 2, ALL)
+        store_result(2, ALL)
+        round_result(1, 2, 1)
         turn_result(1, 0, 2)
         turn_result(1, 2, 1)
         keep_warm(warm[:])
-        log_base(2)
-        log_eps(2)
         quant_result(0, 0)
-        log_series(2)
         quant_result(0, 1)
-        lift("vector", res, 2, ALL)
-        store_result(2, ALL)
-        keep_warm(res[2][:, 0:P])
         quant_result(0, 2)
         store_codes(0, 1)
         log_guess(3)
-        copy_result(1, 2, 1, "scalar")
         log_ratio(3)
         copy_result(1, 0, 2, "scalar")
-        round_result(2, 0, 2)
+        copy_result(1, 2, 1, "scalar")
+        round_result(2, 0, 1)
         log_base(3)
         log_eps(3)
-        round_result(2, 2, 1)
+        round_result(2, 1, 1)
         log_series(3)
+        round_result(2, 2, 1)
         turn_result(2, 0, 2)
         turn_result(2, 2, 1)
         keep_warm(warm[:])
-        quant_result(1, 2)
-        lift("scalar", res, 3, slice(0, 768))
-        store_result(3, slice(0, 768))
-        round_result(3, 0, 2)
-        turn_result(3, 0, 2)
-        round_result(3, 2, 1)
-        turn_result(3, 2, 1)
         lift("vector", res, 3, slice(768, NZ))
         store_result(3, slice(768, NZ))
+        lift("scalar", res, 3, slice(0, 768))
+        store_result(3, slice(0, 768))
+        round_result(3, 0, 3)
+        turn_result(3, 0, 2)
+        turn_result(3, 2, 1)
         copy_result(2, 0, 2, "scalar")
+        copy_result(2, 2, 1, "scalar")
         copy_result(3, 0, 2, "scalar")
         quant_result(1, 0)
         quant_result(1, 1)
+        quant_result(1, 2)
         store_codes(1, 1)
-        copy_result(2, 2, 1, "vector")
         quant_result(2, 0)
-        copy_result(3, 2, 1, "vector")
         quant_result(2, 1)
+        copy_result(3, 2, 1, "vector")
         quant_result(2, 2)
+        store_codes(2, 1)
         quant_result(3, 2)
         quant_result(3, 0)
         quant_result(3, 1)
-        store_codes(2, 2)
+        store_codes(3, 1)
         store_scales(0, nc.scalar)
         store_scales(1, nc.sync)
         store_scales(2, nc.scalar)

@@ -55,7 +55,7 @@ def tile_copynetjointgeneratecopyloglift_x2_kernel(
         wo_codes = keep("wo_codes", [P, 2 * V], U8)
         wo_plane = keep("wo_plane", [P, V], U8)
         g_raw = keep("g_raw", [P, 4], BF16)
-        g4 = keep("g4", [P, 4], F32)
+        gains = keep("gains", [P, BANK], F32)
         bo_raw = keep("bo_raw", [8, P], BF16)
         bo_rows = keep("bo_rows", [P, P], F32)
         bo_cols = keep("bo_cols", [P, 8], F32)
@@ -89,7 +89,7 @@ def tile_copynetjointgeneratecopyloglift_x2_kernel(
         def load_rows(key):
             name, b, half = key
             src = h[b, 256 * half : 256 * half + 256, :] if name == "h" else s[b]
-            nc.sync.dma_start(out=rows[key][:], in_=src.rearrange("(j p) d -> p j d", p=P))
+            nc.sync.dma_start(out=rows[key][:], in_=src.rearrange("(p j) d -> p j d", p=P))
 
         def load_scale_rows(engine, dst, src):
             for q in range(4):
@@ -109,8 +109,8 @@ def tile_copynetjointgeneratecopyloglift_x2_kernel(
         def copy_rows(key, engine):
             copy_on(
                 engine,
-                grouped[key][:].bitcast(F32).rearrange("p (j r u) -> p j r u", j=2, u=2),
-                banks[key][:].rearrange("p (j u r) -> p j r u", j=2, u=2),
+                grouped[key][:].bitcast(F32).rearrange("p (r j u) -> p r j u", j=2, u=2),
+                banks[key][:].rearrange("p (j u r) -> p r j u", j=2, u=2),
             )
 
         def quant_rows(key):
@@ -141,10 +141,7 @@ def tile_copynetjointgeneratecopyloglift_x2_kernel(
         def gain(b, j, engine="vector"):
             c0 = (j % 2) * BANK
             (nc.vector if engine == "vector" else nc.gpsimd).tensor_tensor(
-                out=kb[2 * b + j // 2][:, c0 : c0 + BANK].rearrange("p (n t) -> p n t", t=4),
-                in0=th[4 * b + j][:].rearrange("p (n t) -> p n t", t=4),
-                in1=g4[:].unsqueeze(1).to_broadcast([P, P, 4]),
-                op=ALU.mult,
+                out=kb[2 * b + j // 2][:, c0 : c0 + BANK], in0=th[4 * b + j][:], in1=gains[:], op=ALU.mult
             )
 
         def quant_keys(b, half):
@@ -290,8 +287,8 @@ def tile_copynetjointgeneratecopyloglift_x2_kernel(
                     op1=ALU.add,
                 )
 
-        def keep_warm(src):
-            nc.tensor.matmul(out=banks["warm"][:, 0:P], lhsT=warm[:], rhs=src, start=True, stop=True)
+        def keep_warm():
+            nc.tensor.matmul(out=banks["warm"][:, 0:P], lhsT=warm[:], rhs=warm[:], start=True, stop=True)
 
         def store_result(i, cols):
             nc.sync.dma_start(out=out_0[i // 2, (i % 2) * P : (i % 2) * P + P, cols], in_=res[i][:, cols])
@@ -350,9 +347,9 @@ def tile_copynetjointgeneratecopyloglift_x2_kernel(
         load_rows(H0B)
         load_rows(S0)
         nc.sync.dma_start(out=wo_codes[:].bitcast(I32), in_=wo_words[0].bitcast(I32))
+        nc.sync.dma_start(out=bo_raw[:], in_=bo.rearrange("(c p) -> c p", p=P))
         nc.sync.dma_start(out=g_raw[:], in_=g.rearrange("(p t) -> p t", t=4))
         load_scale_rows(nc.sync, wo_plane, wo_scales)
-        nc.sync.dma_start(out=bo_raw[:], in_=bo.rearrange("(c p) -> c p", p=P))
         load_rows(H1A)
         load_rows(H1B)
         load_rows(S1)
@@ -393,15 +390,17 @@ def tile_copynetjointgeneratecopyloglift_x2_kernel(
             nc.vector.tensor_copy(out=bo_cols[:], in_=banks["bo"][:, 0:8])
 
         def copy_gain():
-            nc.vector.tensor_copy(out=g4[:], in_=g_raw[:])
+            nc.vector.tensor_copy(
+                out=gains[:].rearrange("p (n t) -> p n t", t=4), in_=g_raw[:].unsqueeze(1).to_broadcast([P, P, 4])
+            )
 
         banks["warm"] = bank()
-        keep_warm(warm[:])
-        keep_warm(warm[:])
-        keep_warm(warm[:])
-        keep_warm(warm[:])
+        keep_warm()
+        keep_warm()
+        keep_warm()
+        keep_warm()
         turn_rows(H0A)
-        keep_warm(warm[:])
+        keep_warm()
         copy_rows(H0A, "scalar")
         fill_series()
         turn_rows(H0B)
@@ -415,9 +414,9 @@ def tile_copynetjointgeneratecopyloglift_x2_kernel(
         quant_rows(H0B)
         project(0, 2)
         project(0, 3)
-        copy_gain()
         cast_bias()
         quant_rows(S0)
+        copy_gain()
         turn_bias()
         squash(0, 0)
         generate(0, 0)
@@ -456,63 +455,59 @@ def tile_copynetjointgeneratecopyloglift_x2_kernel(
         turn_scores(0, 1)
         negate_min(0, 0, 0)
         quant_rows(H1B)
+        quant_rows(S1)
         project(1, 2)
         project(1, 3)
-        negate_min(0, 2, 1)
-        quant_rows(S1)
         squash(1, 0)
+        gain(1, 0, "gpsimd")
         squash(1, 1)
+        gain(1, 1, "gpsimd")
+        negate_min(0, 2, 1)
         turn_scores(1, 0)
-        generate(1, 0)
-        generate(1, 1)
+        copy_scores(1)
         squash(1, 2)
         squash(1, 3)
-        gain(1, 0)
         negate_min(0, 1, 2)
+        negate_min(1, 0, 0)
+        generate(1, 0)
+        generate(1, 1)
         generate(1, 2)
-        generate(1, 3)
-        copy_scores(1)
         turn_scores(1, 1)
         exp_sum(0)
-        gain(1, 1)
+        negate_min(1, 2, 1)
+        generate(1, 3)
         gain(1, 2)
         quant_keys(1, 0)
         gain(1, 3)
-        negate_min(1, 0, 0)
-        quant_keys(1, 1)
         add_bias(1, 0)
         log_guess(0)
         add_bias(1, 1)
         log_ratio(0)
         add_bias(1, 2)
         add_bias(1, 3)
-        copy_scores(2)
-        turn_scores(2, 0)
-        turn_scores(3, 0)
         log_base(0)
         log_eps(0)
-        negate_min(1, 2, 1)
+        quant_keys(1, 1)
         log_series(0)
-        copy_scores(3)
         lift("gpsimd", res, 0, ALL)
         store_result(0, ALL)
+        negate_min(1, 1, 2)
+        turn_scores(2, 0)
+        copy_scores(2)
+        copy_scores(3)
         add_bias(1, 4)
         add_bias(1, 5)
         add_bias(1, 6)
         add_bias(1, 7)
         turn_scores(2, 1)
+        turn_scores(3, 0)
         turn_scores(3, 1)
-        banks["warm"] = bank()
-        negate_min(1, 1, 2)
         exp_sum(1)
         negate_min(2, 0, 0)
-        keep_warm(nz[2][:, 0:P])
-        negate_min(3, 0, 0)
+        negate_min(3, 2, 0)
         negate_min(2, 2, 1)
-        keep_warm(nz[2][:, 1024:1152])
         round_result(0, 0, 1)
         negate_min(2, 1, 2)
-        keep_warm(nz[2][:, 512:640])
         log_guess(1)
         log_ratio(1)
         exp_sum(2)
@@ -523,13 +518,13 @@ def tile_copynetjointgeneratecopyloglift_x2_kernel(
         log_series(1)
         turn_result(0, 0, 2)
         turn_result(0, 2, 1)
-        lift("gpsimd", res, 1, ALL)
-        store_result(1, ALL)
-        negate_min(3, 2, 1)
-        keep_warm(nz[3][:, 1024:1152])
+        lift("gpsimd", res, 1, slice(0, 768))
+        store_result(1, slice(0, 768))
+        lift("gpsimd", res, 1, slice(768, NZ))
+        store_result(1, slice(768, NZ))
+        negate_min(3, 0, 1)
         copy_result(0, 0, 2, "vector")
         negate_min(3, 1, 2)
-        keep_warm(nz[3][:, 512:640])
         log_guess(2)
         copy_result(0, 2, 1, "scalar")
         log_ratio(2)
@@ -538,52 +533,49 @@ def tile_copynetjointgeneratecopyloglift_x2_kernel(
         log_eps(2)
         round_result(1, 0, 1)
         log_series(2)
-        round_result(1, 1, 1)
-        lift("vector", res, 2, ALL)
-        store_result(2, ALL)
-        round_result(1, 2, 1)
+        round_result(1, 1, 2)
         turn_result(1, 0, 2)
         turn_result(1, 2, 1)
-        keep_warm(warm[:])
+        lift("vector", res, 2, slice(0, 768))
+        store_result(2, slice(0, 768))
+        lift("vector", res, 2, slice(768, NZ))
+        store_result(2, slice(768, NZ))
+        log_guess(3)
+        copy_result(1, 2, 1, "scalar")
+        log_ratio(3)
+        copy_result(1, 0, 2, "scalar")
         quant_result(0, 0)
+        log_base(3)
+        log_eps(3)
         quant_result(0, 1)
         quant_result(0, 2)
         store_codes(0, 1)
-        log_guess(3)
-        log_ratio(3)
-        copy_result(1, 0, 2, "scalar")
-        copy_result(1, 2, 1, "scalar")
-        round_result(2, 0, 1)
-        log_base(3)
-        log_eps(3)
-        round_result(2, 1, 1)
         log_series(3)
-        round_result(2, 2, 1)
+        round_result(2, 0, 3)
         turn_result(2, 0, 2)
         turn_result(2, 2, 1)
-        keep_warm(warm[:])
-        lift("vector", res, 3, slice(768, NZ))
-        store_result(3, slice(768, NZ))
-        lift("scalar", res, 3, slice(0, 768))
-        store_result(3, slice(0, 768))
+        lift("vector", res, 3, slice(1024, NZ))
+        store_result(3, slice(1024, NZ))
+        lift("scalar", res, 3, slice(0, 1024))
+        store_result(3, slice(0, 1024))
         round_result(3, 0, 3)
         turn_result(3, 0, 2)
         turn_result(3, 2, 1)
         copy_result(2, 0, 2, "scalar")
         copy_result(2, 2, 1, "scalar")
         copy_result(3, 0, 2, "scalar")
+        copy_result(3, 2, 1, "scalar")
         quant_result(1, 0)
         quant_result(1, 1)
         quant_result(1, 2)
         store_codes(1, 1)
         quant_result(2, 0)
         quant_result(2, 1)
-        copy_result(3, 2, 1, "vector")
         quant_result(2, 2)
         store_codes(2, 1)
-        quant_result(3, 2)
         quant_result(3, 0)
         quant_result(3, 1)
+        quant_result(3, 2)
         store_codes(3, 1)
         store_scales(0, nc.scalar)
         store_scales(1, nc.sync)

import math
from contextlib import ExitStack

import concourse.mybir as mybir
from concourse.masks import make_identity

B, S, T, D, V = 2, 256, 512, 512, 1024
NZ = V + T
FLOPS = 2 * B * (T * D * D + S * D * T + S * D * V)

F32 = mybir.dt.float32
BF16 = mybir.dt.bfloat16
I32 = mybir.dt.int32
U32 = mybir.dt.uint32
U8 = mybir.dt.uint8
FP8X4 = mybir.dt.float8_e4m3fn_x4
FP4X4 = mybir.dt.float4_e2m1fn_x4
ACT = mybir.ActivationFunctionType
ALU = mybir.AluOpType

P = 128
BANK = 512
GROUPS = NZ // 512
TILES = B * S // P
LN2 = math.log(2.0)
TERMS = 20


def tile_copynetjointgeneratecopyloglift_x2_kernel(
    tc, h, wc_words, wc_scales, g, s, wo_words, wo_scales, bo, out_0, out_1, out_2
):
    nc = tc.nc
    with ExitStack() as ctx:
        sb = ctx.enter_context(tc.tile_pool(name="sb", bufs=1))
        psum = ctx.enter_context(tc.psum_pool(name="psum", bufs=8))
        ctx.enter_context(tc.manual_schedule())

        def keep(name, shape, dtype):
            return sb.tile(shape, dtype, name=name, align_bytes=64)

        def bank():
            return psum.tile([P, BANK], F32, name="bank")

        def copy_on(engine, out, in_):
            if engine == "scalar":
                nc.scalar.copy(out=out, in_=in_)
            else:
                nc.vector.tensor_copy(out=out, in_=in_)

        ident = keep("ident", [P, P], F32)
        wc_raw = keep("wc_raw", [P, 2 * D], U8)
        wc_sraw = keep("wc_sraw", [P, D], U8)
        wc_codes = keep("wc_codes", [P, 2 * D], U8)
        wc_plane = keep("wc_plane", [P, D], U8)
        wo_codes = keep("wo_codes", [P, 2 * V], U8)
        wo_plane = keep("wo_plane", [P, V], U8)
        g_raw = keep("g_raw", [P, 4], BF16)
        gains = keep("gains", [P, BANK], F32)
        bo_raw = keep("bo_raw", [8, P], BF16)
        bo_rows = keep("bo_rows", [P, P], F32)
        bo_cols = keep("bo_cols", [P, 8], F32)
        series = keep("series", [P, TILES, TERMS + 4], F32)
        count = keep("count", [P, TERMS], F32)
        inverse = keep("inverse", [P, TERMS], F32)
        warm = keep("warm", [P, P], F32)
        table = keep("table", [P, 8], F32)
        rows = {}
        for key in [("h", 0, 0), ("h", 0, 1), ("s", 0, 0), ("h", 1, 0), ("h", 1, 1), ("s", 1, 0)]:
            rows[key] = keep("rows_%s%d%d" % key, [P, 2, D], BF16)
        grouped = {key: keep("grp_%s%d%d" % key, [P, 1024], BF16) for key in rows}
        codes = {key: keep("cod_%s%d%d" % key, [P, 256], U32) for key in rows}
        plane = {key: keep("pln_%s%d%d" % key, [P, 256], U8) for key in rows}
        th = [keep("th%d" % i, [P, BANK], F32) for i in range(8)]
        kb = [keep("kb%d" % i, [P, 1024], BF16) for i in range(4)]
        k_codes = [keep("kc%d" % b, [P, T], U32) for b in range(B)]
        k_plane = [keep("kp%d" % b, [P, T], U8) for b in range(B)]
        gen_t = [keep("gent%d" % b, [P, 8, S], F32) for b in range(B)]
        nz = [keep("nz%d" % i, [P, NZ], F32) for i in range(TILES)]
        stats = [keep("st%d" % i, [P, 16], F32) for i in range(TILES)]
        horner = [keep("hn%d" % i, [P, TERMS + 4], F32) for i in range(TILES)]
        junk = [keep("junk%d" % i, [P, NZ], BF16) for i in range(2)]
        res = [keep("res%d" % i, [P, NZ], F32) for i in range(TILES)]
        res_b = [keep("resb%d" % i, [P, NZ], BF16) for i in range(TILES)]
        res_g = [keep("resg%d" % i, [P, NZ], BF16) for i in range(TILES)]
        o_codes = keep("o_codes", [P, GROUPS, B * S], U32)
        o_plane = keep("o_plane", [P, GROUPS, B * S], U8)
        banks = {}

        def load_rows(key):
            name, b, half = key
            src = h[b, 256 * half : 256 * half + 256, :] if name == "h" else s[b]
            nc.sync.dma_start(out=rows[key][:], in_=src.rearrange("(p j) d -> p j d", p=P))

        def load_scale_rows(engine, dst, src):
            for q in range(4):
                engine.dma_start(
                    out=dst[32 * q : 32 * q + 4, :].bitcast(I32),
                    in_=src[0, 4 * q : 4 * q + 4, :].bitcast(I32),
                )

        def turn_rows(key):
            banks[key] = bank()
            for j in range(2):
                words = rows[key][:, j, :].bitcast(F32)
                for u in range(2):
                    c0 = (2 * j + u) * P
                    nc.tensor.transpose(banks[key][:, c0 : c0 + P], words[:, u::2], ident[:])

        def copy_rows(key, engine):
            copy_on(
                engine,
                grouped[key][:].bitcast(F32).rearrange("p (r j u) -> p r j u", j=2, u=2),
                banks[key][:].rearrange("p (j u r) -> p r j u", j=2, u=2),
            )

        def quant_rows(key):
            nc.vector.quantize_mx(out=codes[key][:].bitcast(FP8X4), scales=plane[key][:], in_=grouped[key][:])

        def project(b, j):
            key = ("h", b, j // 2)
            cols = slice((j % 2) * P, (j % 2) * P + P)
            banks["p", b, j] = bank()
            for t in range(4):
                nc.tensor.matmul_mx(
                    out=banks["p", b, j][:, t * P : (t + 1) * P],
                    lhsT=wc_codes[:, 2 * P * t : 2 * P * (t + 1)].bitcast(FP4X4),
                    lhsT_scale=wc_plane[:, P * t : P * (t + 1)],
                    rhs=codes[key][:, cols].bitcast(FP8X4),
                    rhs_scale=plane[key][:, cols],
                    start=True,
                    stop=True,
                )

        def squash(b, j):
            nc.scalar.activation(
                out=th[4 * b + j][:].rearrange("p (n t) -> p n t", t=4),
                in_=banks["p", b, j][:].rearrange("p (t n) -> p n t", t=4),
                func=ACT.Tanh,
            )

        def gain(b, j, engine="vector"):
            c0 = (j % 2) * BANK
            (nc.vector if engine == "vector" else nc.gpsimd).tensor_tensor(
                out=kb[2 * b + j // 2][:, c0 : c0 + BANK], in0=th[4 * b + j][:], in1=gains[:], op=ALU.mult
            )

        def quant_keys(b, half):
            cols = slice(256 * half, 256 * half + 256)
            nc.vector.quantize_mx(
                out=k_codes[b][:, cols].bitcast(FP8X4), scales=k_plane[b][:, cols], in_=kb[2 * b + half][:]
            )

        def generate(b, pair):
            key = ("s", b, 0)
            banks["g", b, pair] = bank()
            for e in range(2):
                c = 2 * pair + e
                nc.tensor.matmul_mx(
                    out=banks["g", b, pair][:, e * S : (e + 1) * S],
                    lhsT=wo_codes[:, 2 * P * c : 2 * P * (c + 1)].bitcast(FP4X4),
                    lhsT_scale=wo_plane[:, P * c : P * (c + 1)],
                    rhs=codes[key][:].bitcast(FP8X4),
                    rhs_scale=plane[key][:],
                    start=True,
                    stop=True,
                )

        def add_bias(b, c, engine="scalar"):
            src = banks["g", b, c // 2][:, (c % 2) * S : (c % 2 + 1) * S]
            if engine == "scalar":
                nc.scalar.activation(out=gen_t[b][:, c, :], in_=src, func=ACT.Identity, bias=bo_cols[:, c : c + 1])
            else:
                nc.vector.tensor_scalar(
                    out=gen_t[b][:, c, :], in0=src, scalar1=bo_cols[:, c : c + 1], scalar2=None, op0=ALU.add
                )

        def turn_scores(i, half):
            b, r0 = i // 2, (i % 2) * P
            banks["z", i, half] = bank()
            for e in range(4):
                nc.tensor.transpose(
                    banks["z", i, half][:, e * P : (e + 1) * P], gen_t[b][:, 4 * half + e, r0 : r0 + P], ident[:]
                )

        def copy_scores(i):
            b = i // 2
            cols = slice((i % 2) * P, (i % 2) * P + P)
            banks["z", i, 2] = bank()
            nc.tensor.matmul_mx(
                out=banks["z", i, 2][:],
                lhsT=codes["s", b, 0][:, cols].bitcast(FP8X4),
                lhsT_scale=plane["s", b, 0][:, cols],
                rhs=k_codes[b][:].bitcast(FP8X4),
                rhs_scale=k_plane[b][:],
                start=True,
                stop=True,
            )

        def negate_min(i, part, col):
            factor = -1.0 / math.sqrt(D) if part == 2 else -1.0
            nc.vector.tensor_scalar(
                out=nz[i][:, part * BANK : (part + 1) * BANK],
                in0=banks["z", i, part][:],
                scalar1=factor,
                scalar2=None if col == 0 else stats[i][:, col - 1 : col],
                op0=ALU.mult,
                op1=ALU.min,
                accum_out=stats[i][:, col : col + 1],
            )

        def exp_sum(i):
            nc.scalar.activation(
                out=junk[i % 2][:],
                in_=nz[i][:],
                func=ACT.Exp,
                scale=-1.0,
                bias=stats[i][:, 2:3],
                accum_out=stats[i][:, 3:4],
            )

        def log_guess(i):
            nc.scalar.activation(
                out=stats[i][:, 4:5],
                in_=stats[i][:, 3:4].bitcast(U32),
                func=ACT.Copy,
                scale=-LN2 / 2.0**23,
                bias=(127.0 - 0.043) * LN2,
            )

        def log_ratio(i):
            nc.scalar.activation(out=stats[i][:, 5:6], in_=stats[i][:, 4:5], func=ACT.Exp)

        def log_base(i):
            nc.vector.tensor_scalar(
                out=series[:, i, TERMS : TERMS + 1],
                in0=stats[i][:, 4:5],
                scalar1=stats[i][:, 2:3],
                scalar2=math.log(NZ),
                op0=ALU.add,
                op1=ALU.add,
            )

        def log_eps(i):
            nc.vector.tensor_scalar(
                out=stats[i][:, 6:7],
                in0=stats[i][:, 3:4],
                scalar1=stats[i][:, 5:6],
                scalar2=-1.0,
                op0=ALU.mult,
                op1=ALU.add,
            )

        def log_series(i):
            nc.vector.tensor_tensor_scan(
                out=horner[i][:, 0 : TERMS + 1],
                data0=stats[i][:, 6:7].to_broadcast([P, TERMS + 1]),
                data1=series[:, i, 0 : TERMS + 1],
                initial=0.0,
                op0=ALU.mult,
                op1=ALU.add,
            )

        def lift(engine, dst, i, cols):
            if engine == "scalar":
                nc.scalar.activation(
                    out=dst[i][:, cols], in_=nz[i][:, cols], func=ACT.Identity, scale=-1.0, bias=horner[i][:, TERMS : TERMS + 1]
                )
            else:
                (nc.vector if engine == "vector" else nc.gpsimd).tensor_scalar(
                    out=dst[i][:, cols],
                    in0=nz[i][:, cols],
                    scalar1=-1.0,
                    scalar2=horner[i][:, TERMS : TERMS + 1],
                    op0=ALU.mult,
                    op1=ALU.add,
                )

        def round_result(i, first, count):
            for gg in range(first, first + count):
                cols = slice(512 * gg, 512 * (gg + 1))
                nc.vector.tensor_scalar(
                    out=res_b[i][:, cols].rearrange("p (u w e) -> p u w e", u=2, e=2),
                    in0=nz[i][:, cols].rearrange("p (w u e) -> p u w e", u=2, e=2),
                    scalar1=-1.0,
                    scalar2=horner[i][:, TERMS : TERMS + 1],
                    op0=ALU.mult,
                    op1=ALU.add,
                )

        def keep_warm():
            nc.tensor.matmul(out=banks["warm"][:, 0:P], lhsT=warm[:], rhs=warm[:], start=True, stop=True)

        def store_result(i, cols):
            nc.sync.dma_start(out=out_0[i // 2, (i % 2) * P : (i % 2) * P + P, cols], in_=res[i][:, cols])

        def turn_result(i, first, count):
            banks["o", i, first] = bank()
            words = res_b[i][:].bitcast(F32)
            for gg in range(count):
                for u in range(2):
                    c0 = (2 * gg + u) * P
                    w0 = 256 * (first + gg)
                    nc.tensor.transpose(
                        banks["o", i, first][:, c0 : c0 + P], words[:, w0 + u * P : w0 + (u + 1) * P], ident[:]
                    )

        def copy_result(i, first, count, engine):
            copy_on(
                engine,
                res_g[i][:, 512 * first : 512 * (first + count)]
                .bitcast(F32)
                .rearrange("p (j r u) -> p j r u", j=count, u=2),
                banks["o", i, first][:, 0 : 256 * count].rearrange("p (j u r) -> p j r u", j=count, u=2),
            )

        def quant_result(i, gg):
            cols = slice(i * P, i * P + P)
            nc.vector.quantize_mx(
                out=o_codes[:, gg, cols].bitcast(FP8X4),
                scales=o_plane[:, gg, cols],
                in_=res_g[i][:, 512 * gg : 512 * (gg + 1)],
            )

        def store_codes(first, count):
            cols = slice(first * P, (first + count) * P)
            dst = out_1.rearrange("g p m t -> p g (m t)").bitcast(I32)
            nc.sync.dma_start(out=dst[:, :, cols], in_=o_codes[:, :, cols].bitcast(I32))

        def store_scales(q, engine):
            engine.dma_start(
                out=out_2[:, 4 * q : 4 * q + 4, :].rearrange("g r m -> r g m").bitcast(I32),
                in_=o_plane[32 * q : 32 * q + 4, :, :].bitcast(I32),
            )

        ALL = slice(0, NZ)
        H0A, H0B, S0, H1A, H1B, S1 = list(rows)

        nc.vector.memset(warm[:], 0.0)
        nc.scalar.activation(out=table[:, 0:1], in_=warm[:, 0:1], func=ACT.Tanh)
        nc.gpsimd.memset(wc_sraw[:].bitcast(I32), 0)
        make_identity(nc, ident[:])
        nc.gpsimd.memset(wo_plane[:].bitcast(I32), 0)
        nc.vector.memset(bo_rows[:], 0.0)
        load_rows(H0A)
        nc.sync.dma_start(out=wc_raw[:].bitcast(I32), in_=wc_words[0].bitcast(I32))
        load_scale_rows(nc.sync, wc_sraw, wc_scales)
        load_rows(H0B)
        load_rows(S0)
        nc.sync.dma_start(out=wo_codes[:].bitcast(I32), in_=wo_words[0].bitcast(I32))
        nc.sync.dma_start(out=bo_raw[:], in_=bo.rearrange("(c p) -> c p", p=P))
        nc.sync.dma_start(out=g_raw[:], in_=g.rearrange("(p t) -> p t", t=4))
        load_scale_rows(nc.sync, wo_plane, wo_scales)
        load_rows(H1A)
        load_rows(H1B)
        load_rows(S1)
        nc.gpsimd.iota(
            count[:], pattern=[[-1, TERMS]], base=TERMS, channel_multiplier=0, allow_small_or_imprecise_dtypes=True
        )

        nc.vector.tensor_copy(
            out=wc_codes[:].rearrange("p (t m e) -> p t m e", t=4, e=2),
            in_=wc_raw[:].rearrange("p (m t e) -> p t m e", t=4, e=2),
        )
        nc.vector.tensor_copy(
            out=wc_plane[:].rearrange("p (t m) -> p t m", t=4),
            in_=wc_sraw[:].rearrange("p (m t) -> p t m", t=4),
        )

        def fill_series():
            nc.vector.reciprocal(out=inverse[:], in_=count[:])

        def sign_series():
            for first, factor in [(0, 1.0), (1, -1.0)]:
                nc.vector.tensor_scalar(
                    out=series[:, :, first:TERMS:2],
                    in0=inverse[:, first:TERMS:2].unsqueeze(1).to_broadcast([P, TILES, TERMS // 2]),
                    scalar1=factor,
                    scalar2=None,
                    op0=ALU.mult,
                )

        def cast_bias():
            nc.vector.tensor_copy(out=bo_rows[0:8, :], in_=bo_raw[:])

        def turn_bias():
            banks["bo"] = bank()
            nc.tensor.transpose(banks["bo"][:, 0:P], bo_rows[:], ident[:])

        def copy_bias():
            nc.vector.tensor_copy(out=bo_cols[:], in_=banks["bo"][:, 0:8])

        def copy_gain():
            nc.vector.tensor_copy(
                out=gains[:].rearrange("p (n t) -> p n t", t=4), in_=g_raw[:].unsqueeze(1).to_broadcast([P, P, 4])
            )

        banks["warm"] = bank()
        keep_warm()
        keep_warm()
        keep_warm()
        keep_warm()
        turn_rows(H0A)
        keep_warm()
        copy_rows(H0A, "scalar")
        fill_series()
        turn_rows(H0B)
        quant_rows(H0A)
        copy_rows(H0B, "vector")
        turn_rows(S0)
        project(0, 0)
        project(0, 1)
        copy_rows(S0, "scalar")
        sign_series()
        quant_rows(H0B)
        project(0, 2)
        project(0, 3)
        cast_bias()
        quant_rows(S0)
        copy_gain()
        turn_bias()
        squash(0, 0)
        generate(0, 0)
        generate(0, 1)
        squash(0, 1)
        gain(0, 0)
        copy_bias()
        turn_rows(H1A)
        squash(0, 2)
        generate(0, 2)
        gain(0, 1)
        squash(0, 3)
        turn_rows(H1B)
        generate(0, 3)
        gain(0, 2)
        quant_keys(0, 0)
        gain(0, 3)
        add_bias(0, 0)
        add_bias(0, 1)
        add_bias(0, 2)
        add_bias(0, 3)
        copy_rows(H1A, "vector")
        quant_keys(0, 1)
        turn_rows(S1)
        turn_scores(0, 0)
        quant_rows(H1A)
        copy_rows(H1B, "vector")
        project(1, 0)
        project(1, 1)
        copy_scores(0)
        add_bias(0, 4)
        add_bias(0, 5)
        add_bias(0, 6)
        add_bias(0, 7)
        copy_rows(S1, "scalar")
        turn_scores(0, 1)
        negate_min(0, 0, 0)
        quant_rows(H1B)
        quant_rows(S1)
        project(1, 2)
        project(1, 3)
        squash(1, 0)
        gain(1, 0, "gpsimd")
        squash(1, 1)
        gain(1, 1, "gpsimd")
        negate_min(0, 2, 1)
        turn_scores(1, 0)
        copy_scores(1)
        squash(1, 2)
        squash(1, 3)
        negate_min(0, 1, 2)
        negate_min(1, 0, 0)
        generate(1, 0)
        generate(1, 1)
        generate(1, 2)
        turn_scores(1, 1)
        exp_sum(0)
        negate_min(1, 2, 1)
        generate(1, 3)
        gain(1, 2)
        quant_keys(1, 0)
        gain(1, 3)
        add_bias(1, 0)
        log_guess(0)
        add_bias(1, 1)
        log_ratio(0)
        add_bias(1, 2)
        add_bias(1, 3)
        log_base(0)
        log_eps(0)
        quant_keys(1, 1)
        log_series(0)
        lift("gpsimd", res, 0, ALL)
        store_result(0, ALL)
        negate_min(1, 1, 2)
        turn_scores(2, 0)
        copy_scores(2)
        copy_scores(3)
        add_bias(1, 4)
        add_bias(1, 5)
        add_bias(1, 6)
        add_bias(1, 7)
        turn_scores(2, 1)
        turn_scores(3, 0)
        turn_scores(3, 1)
        exp_sum(1)
        negate_min(2, 0, 0)
        negate_min(3, 2, 0)
        negate_min(2, 2, 1)
        round_result(0, 0, 1)
        negate_min(2, 1, 2)
        log_guess(1)
        log_ratio(1)
        exp_sum(2)
        round_result(0, 1, 1)
        log_base(1)
        log_eps(1)
        round_result(0, 2, 1)
        log_series(1)
        turn_result(0, 0, 2)
        turn_result(0, 2, 1)
        lift("gpsimd", res, 1, slice(0, 768))
        store_result(1, slice(0, 768))
        lift("gpsimd", res, 1, slice(768, NZ))
        store_result(1, slice(768, NZ))
        negate_min(3, 0, 1)
        copy_result(0, 0, 2, "vector")
        negate_min(3, 1, 2)
        log_guess(2)
        copy_result(0, 2, 1, "scalar")
        log_ratio(2)
        exp_sum(3)
        log_base(2)
        log_eps(2)
        round_result(1, 0, 1)
        log_series(2)
        round_result(1, 1, 2)
        turn_result(1, 0, 2)
        turn_result(1, 2, 1)
        lift("vector", res, 2, slice(0, 768))
        store_result(2, slice(0, 768))
        lift("vector", res, 2, slice(768, NZ))
        store_result(2, slice(768, NZ))
        log_guess(3)
        copy_result(1, 2, 1, "scalar")
        log_ratio(3)
        copy_result(1, 0, 2, "scalar")
        quant_result(0, 0)
        log_base(3)
        log_eps(3)
        quant_result(0, 1)
        quant_result(0, 2)
        store_codes(0, 1)
        log_series(3)
        round_result(2, 0, 3)
        turn_result(2, 0, 2)
        turn_result(2, 2, 1)
        lift("vector", res, 3, slice(1024, NZ))
        store_result(3, slice(1024, NZ))
        lift("scalar", res, 3, slice(0, 1024))
        store_result(3, slice(0, 1024))
        round_result(3, 0, 3)
        turn_result(3, 0, 2)
        turn_result(3, 2, 1)
        copy_result(2, 0, 2, "scalar")
        copy_result(2, 2, 1, "scalar")
        copy_result(3, 0, 2, "scalar")
        copy_result(3, 2, 1, "scalar")
        quant_result(1, 0)
        quant_result(1, 1)
        quant_result(1, 2)
        store_codes(1, 1)
        quant_result(2, 0)
        quant_result(2, 1)
        quant_result(2, 2)
        store_codes(2, 1)
        quant_result(3, 0)
        quant_result(3, 1)
        quant_result(3, 2)
        store_codes(3, 1)
        store_scales(0, nc.scalar)
        store_scales(1, nc.sync)
        store_scales(2, nc.scalar)
        store_scales(3, nc.sync)
